import numpy as np
import ml_dtypes


def mxq(x, axis, fmt="e4m3"):
    dtype, down = {"e4m3": (ml_dtypes.float8_e4m3fn, 7), "e5m2": (ml_dtypes.float8_e5m2, 14)}[fmt]
    v = np.moveaxis(np.asarray(x, np.float32).astype(ml_dtypes.bfloat16).astype(np.float64), axis, -1)
    blocks = v.reshape(v.shape[:-1] + (-1, 32))
    amax = np.abs(blocks).max(-1, keepdims=True)
    byte = np.maximum(np.where(amax > 0, np.frexp(amax)[1] - 1 + 127, 0) - down, 1)
    scale = np.exp2(byte - 127.0)
    codes = (blocks / scale).astype(np.float32).astype(dtype).astype(np.float64)
    return np.moveaxis((codes * scale).reshape(v.shape), -1, axis)


WIDE = False


def mx_kscale(k):
    if not WIDE:
        return np.ones(k)
    levels = np.array([10, -10, 5, -5, 0])
    if k % 512:
        return np.exp2(np.random.permutation(np.resize(levels, k // 32))).repeat(32)
    a = np.empty((k // 512, 16))
    for p in range(k // 512):
        a[p, :8] = np.random.permutation(np.resize(levels, 8))
        for g in range(8):
            far = levels[np.abs(levels - a[p, g]) >= 10]
            a[p, g + 8] = far[np.random.randint(len(far))]
    return np.exp2(a.ravel()).repeat(32)


def f64(x):
    return np.asarray(x).astype(np.float64)


def striped(idx):
    return np.tile(np.asarray(idx).reshape(-1, 16).T, (8, 1)).astype(np.uint16)


def unstriped(offs):
    return offs[:16].T.reshape(-1).astype(np.int64)


E2M1 = np.array([0.0, 0.5, 1.0, 1.5, 2.0, 3.0, 4.0, 6.0, -0.0, -0.5, -1.0, -1.5, -2.0, -3.0, -4.0, -6.0])


def pack_weight(w, fmt):
    k, n = w.shape
    w = f64(np.asarray(w, np.float32).astype(ml_dtypes.bfloat16)).reshape(k // 32, 32, n)
    amax = np.abs(w).max(1)
    if fmt == "e4m3":
        byte = np.frexp(amax)[1] - 1 + 127 - 7
    else:
        mant, ex = np.frexp(amax / 6.0)
        byte = np.where(mant > 0.5, ex, ex - 1) + 127
    byte = np.clip(np.where(amax > 0, byte, 1), 1, 254)
    scaled = (w * np.exp2(127.0 - byte)[:, None, :]).reshape(k, n).astype(np.float32)
    by_word = np.ascontiguousarray(scaled.reshape(k // 512, 128, 4, n).transpose(0, 1, 3, 2))
    if fmt == "e4m3":
        words = by_word.astype(ml_dtypes.float8_e4m3fn).view(np.uint8)
    else:
        c = by_word.astype(ml_dtypes.float4_e2m1fn).view(np.uint8) & 0xF
        words = (c[..., 0::2] | (c[..., 1::2] << 4)).reshape(k // 512, 128, 2 * n)
    return np.ascontiguousarray(words), np.ascontiguousarray(byte.astype(np.uint8).reshape(k // 512, 16, n))


def unpack_weight(words, scales, fmt):
    g, _, n = scales.shape
    words = np.ascontiguousarray(words).reshape(g, 128, n, -1)
    if fmt == "e4m3":
        vals = words.view(ml_dtypes.float8_e4m3fn).astype(np.float64)
    else:
        nib = np.empty((g, 128, n, 4), np.uint8)
        nib[..., 0::2] = words & 0xF
        nib[..., 1::2] = words >> 4
        vals = E2M1[nib]
    vals = vals * np.repeat(np.exp2(scales.astype(np.float64) - 127.0), 8, axis=1)[..., None]
    return vals.transpose(0, 1, 3, 2).reshape(g * 512, n)


D, E, T, I, Q, G = 512, 512, 2048, 512, 128, 64


def setup_inputs():
    n = np.random.standard_normal
    idx = np.random.permutation(T)[:I]
    fd = mx_kscale(D)
    fe = mx_kscale(E)
    keysp = pack_weight(n((D, T)) / fd[:, None], "e4m3")
    valsp = pack_weight(n((E, T)) / fe[:, None], "e4m3")
    return {
        "query": (n((D, Q)) * 0.8 / np.sqrt(D) * fd[:, None]).astype(np.float32),
        "query2": (n((D, Q)) * 0.8 / np.sqrt(D) * fd[:, None]).astype(np.float32),
        "keys_words": keysp[0],
        "keys_scales": keysp[1],
        "gout": (n((E, Q)) * 1 / np.sqrt(E) * fe[:, None]).astype(np.float32),
        "vals_words": valsp[0],
        "vals_scales": valsp[1],
        "base": (0.5 * n((Q, I))).astype(np.float32),
        "offs": striped(idx),
    }


def reference(query, query2, keys_words, keys_scales, gout, vals_words, vals_scales, base, offs):
    idx = unstriped(offs)
    keysu = unpack_weight(keys_words, keys_scales, "e4m3")
    valsu = unpack_weight(vals_words, vals_scales, "e4m3")
    queryq = mxq(f64(query), 0, "e4m3")
    keysidxg = keysu[:, idx]
    a = queryq.T @ keysidxg
    query2q = mxq(f64(query2), 0, "e4m3")
    b = query2q.T @ keysidxg
    pa = np.exp(a)
    sa = pa.reshape(Q, G, I // G).sum(axis=2)
    z = np.sum(sa, axis=1, keepdims=True)
    pb = np.exp(b)
    sb = pb.reshape(Q, G, I // G).sum(axis=2)
    goutq = mxq(f64(gout), 0, "e4m3")
    valsidxg = valsu[:, idx]
    c0 = goutq.T @ valsidxg
    drr = c0 * pb
    dr = drr.reshape(Q, G, I // G).sum(axis=2)
    dz = np.sum(dr / sb * sa / np.square(z) * (-1.0), axis=1, keepdims=True)
    dsa = dr / sb / z + dz
    r1 = np.repeat(dsa, I // G, axis=1)
    da = r1 * pa
    hda = da * 512.0 * 2.0 * 512.0
    hr1 = hda * pa
    hdsa = hr1.reshape(Q, G, I // G).sum(axis=2)
    hdz = np.sum(hdsa, axis=1, keepdims=True)
    hz = np.sum(hdsa * dr / sb / np.square(z) * (-1.0), axis=1, keepdims=True) + np.sum(hdz * (-1.0) * dr / sb * sa / np.square(np.square(z)) * (-1.0), axis=1, keepdims=True) * z * 2.0
    hsa = hdz * (-1.0) / np.square(z) * dr / sb + hz
    r51 = np.repeat(hsa, I // G, axis=1)
    hpa = hda * r1 + r51
    ha = hpa * pa
    y = ha + f64(base)
    return y

@@ -1,0 +1,212 @@
+import math
+from contextlib import ExitStack
+
+import concourse.mybir as mybir
+from concourse.masks import make_identity
+
+D, E, T, I, Q, G = 512, 512, 2048, 512, 128, 64
+PAGE = I // G
+FLOPS = 3 * 2 * 512 * Q * I
+
+F32 = mybir.dt.float32
+BF16 = mybir.dt.bfloat16
+I32 = mybir.dt.int32
+U32 = mybir.dt.uint32
+U16 = mybir.dt.uint16
+U8 = mybir.dt.uint8
+FP8X4 = mybir.dt.float8_e4m3fn_x4
+ALU = mybir.AluOpType
+ACT = mybir.ActivationFunctionType
+AX = mybir.AxisListType
+
+P = 128
+PACK = 4
+ROOT_C = math.sqrt(512.0 * 2.0 * 512.0)
+
+
+def tile_attend_gppagethensecond_kernel(
+    tc, query, query2, keys_words, keys_scales, gout, vals_words, vals_scales, base, offs, out
+):
+    nc = tc.nc
+    with ExitStack() as ctx:
+        sb = ctx.enter_context(tc.tile_pool(name="sb", bufs=1))
+        ps = ctx.enter_context(tc.psum_pool(name="ps", bufs=1))
+
+        offsets = sb.tile([P, I // 16], U16, name="offsets")
+        key_bytes = sb.tile([P, T], U8, name="key_bytes")
+        val_bytes = sb.tile([P, T], U8, name="val_bytes")
+        key_words = sb.tile([P, T], I32, name="key_words")
+        val_words = sb.tile([P, T], I32, name="val_words", tag="val_words")
+        q1_raw = sb.tile([P, PACK * Q], F32, name="q1_raw")
+        q2_raw = sb.tile([P, PACK * Q], F32, name="q2_raw")
+        g_raw = sb.tile([P, PACK * Q], F32, name="g_raw")
+        base_sb = sb.tile([P, I], F32, name="base_sb")
+
+        nc.vector.memset(val_bytes[:].bitcast(I32), 0)
+        ident = sb.tile([P, P], F32, name="ident")
+        make_identity(nc, ident[:])
+
+        nc.sync.dma_start(offsets[:], offs)
+        key_rows = keys_scales[0].bitcast(I32)
+        for quad in range(4):
+            nc.sync.dma_start(
+                out=key_bytes[32 * quad : 32 * quad + 32, :].bitcast(I32),
+                in_=key_rows[4 * quad : 4 * quad + 4, :].unsqueeze(0).to_broadcast([8, 4, T // 4]),
+            )
+        nc.sync.dma_start(out=q1_raw[:], in_=query.rearrange("(p j) w -> p (j w)", j=PACK))
+        nc.sync.dma_start(out=key_words[:], in_=keys_words[0].rearrange("p n t -> p (n t)").bitcast(I32))
+        nc.sync.dma_start(out=q2_raw[:], in_=query2.rearrange("(p j) w -> p (j w)", j=PACK))
+        nc.sync.dma_start(out=g_raw[:], in_=gout.rearrange("(p j) w -> p (j w)", j=PACK))
+        val_rows = vals_scales[0].bitcast(I32)
+        for quad in range(4):
+            nc.sync.dma_start(
+                out=val_bytes[32 * quad : 32 * quad + 4, :].bitcast(I32),
+                in_=val_rows[4 * quad : 4 * quad + 4, :],
+            )
+        nc.sync.dma_start(out=val_words[:], in_=vals_words[0].rearrange("p n t -> p (n t)").bitcast(I32))
+        nc.sync.dma_start(out=base_sb[:], in_=base)
+
+        def interleave(name, raw):
+            grouped = sb.tile([P, Q * PACK], BF16, name=name + "_bf", align_bytes=64)
+            nc.scalar.copy(
+                out=grouped[:].rearrange("p (w j) -> p w j", j=PACK),
+                in_=raw[:].rearrange("p (j w) -> p w j", j=PACK),
+            )
+            return grouped
+
+        def quantise(name, grouped):
+            codes = sb.tile([P, Q], U32, name=name + "_codes", align_bytes=64)
+            scales = sb.tile([P, Q], U8, name=name + "_scales", align_bytes=64)
+            nc.vector.quantize_mx(out=codes[:].bitcast(FP8X4), scales=scales[:], in_=grouped[:])
+            return codes, scales
+
+        def product(name, rows, words, scale_bytes):
+            acc = ps.tile([P, I], F32, name=name)
+            nc.tensor.matmul_mx(
+                out=acc[:], lhsT=rows[0][:].bitcast(FP8X4), lhsT_scale=rows[1][:],
+                rhs=words[:].bitcast(FP8X4), rhs_scale=scale_bytes[:], start=True, stop=True,
+            )
+            return acc
+
+        q1_bf = interleave("q1", q1_raw)
+        q2_bf = interleave("q2", q2_raw)
+        g_bf = interleave("g", g_raw)
+
+        kb = sb.tile([P, I], U8, name="kb", align_bytes=64)
+        kw = sb.tile([P, I], U32, name="kw", align_bytes=64)
+        vb = sb.tile([P, I], U8, name="vb", align_bytes=64)
+        vw = sb.tile([P, I], U32, name="vw", align_bytes=64)
+
+        nc.vector.tensor_copy(kb[:], key_bytes[:].indirect(offsets[:]))
+        q1_mx = quantise("q1", q1_bf)
+        nc.vector.tensor_copy(kw[:], key_words[:].bitcast(U32).indirect(offsets[:]))
+        a_ps = product("a_ps", q1_mx, kw, kb)
+        q2_mx = quantise("q2", q2_bf)
+        b_ps = product("b_ps", q2_mx, kw, kb)
+
+        def pages(ap):
+            return ap.rearrange("p (g j) -> p g j", j=PAGE)
+
+        def spread(ap):
+            return ap.unsqueeze(2).to_broadcast([P, ap.shape[1], PAGE])
+
+        neg_max = sb.tile([P, 1], F32, name="neg_max")
+        nc.vector.tensor_reduce(out=neg_max[:], in_=a_ps[:], axis=AX.X, op=ALU.max, negate=True)
+        page_max = sb.tile([P, G], F32, name="page_max")
+        nc.vector.tensor_reduce(out=page_max[:], in_=pages(b_ps[:]), axis=AX.X, op=ALU.max)
+        b_rel = sb.tile([P, I], F32, name="b_rel")
+        nc.vector.tensor_tensor(out=pages(b_rel[:]), in0=pages(b_ps[:]), in1=spread(page_max[:]), op=ALU.subtract)
+
+        ee = sb.tile([P, PAGE, 2 * G], F32, name="ee")
+        z = sb.tile([P, 1], F32, name="z")
+        nc.scalar.activation(
+            out=ee[:, :, :G], in_=a_ps[:].rearrange("p (g j) -> p j g", j=PAGE), func=ACT.Exp,
+            bias=neg_max[:], accum_out=z[:],
+        )
+        nc.scalar.activation(out=ee[:, :, G:], in_=ee[:, :, :G], func=ACT.Square)
+        pb = sb.tile([P, I], F32, name="pb")
+        nc.scalar.activation(out=pb[:], in_=b_rel[:], func=ACT.Exp)
+
+        nc.vector.tensor_copy(vb[:], val_bytes[:].indirect(offsets[:]))
+        g_mx = quantise("g", g_bf)
+        nc.vector.tensor_copy(vw[:], val_words[:].bitcast(U32).indirect(offsets[:]))
+        c_ps = product("c_ps", g_mx, vw, vb)
+
+        r = sb.tile([P, 1], F32, name="r")
+        nc.vector.reciprocal(out=r[:], in_=z[:])
+        e_factor = sb.tile([P, 1], F32, name="e_factor")
+        t_factor = sb.tile([P, 1], F32, name="t_factor")
+        nc.gpsimd.tensor_scalar(out=e_factor[:], in0=r[:], scalar1=-2.0 * ROOT_C, scalar2=1.0, op0=ALU.mult, op1=ALU.mult)
+        nc.gpsimd.tensor_scalar(out=t_factor[:], in0=r[:], scalar1=r[:], scalar2=0.5 * ROOT_C, op0=ALU.mult, op1=ALU.mult)
+        e_scaled = sb.tile([P, I], F32, name="e_scaled")
+        nc.scalar.activation(
+            out=pages(e_scaled[:]), in_=ee[:, :, :G].rearrange("p j g -> p g j"), func=ACT.Identity, scale=e_factor[:]
+        )
+
+        turned_ps = ps.tile([P, P], F32, name="turned_ps")
+        for j in range(PAGE):
+            nc.tensor.matmul(
+                turned_ps[:], lhsT=ee[:, j, :], rhs=ident[:], is_transpose=True, start=(j == 0), stop=(j == PAGE - 1)
+            )
+        turned = sb.tile([P, P], F32, name="turned")
+        nc.scalar.copy(out=turned[:], in_=turned_ps[:])
+        sums = ps.tile([P, 2 * G], F32, name="sums")
+        nc.tensor.transpose(sums[:], turned[:], ident[:])
+        t_scaled = sb.tile([P, G], F32, name="t_scaled")
+        nc.scalar.activation(out=t_scaled[:], in_=sums[:, G:], func=ACT.Identity, scale=t_factor[:])
+
+        sum_b = sb.tile([P, G], F32, name="sum_b", tag="val_words")
+        nc.vector.tensor_reduce(out=sum_b[:], in_=pages(pb[:]), axis=AX.X, op=ALU.add)
+        drr = sb.tile([P, I], F32, name="drr")
+        nc.vector.tensor_tensor(out=drr[:], in0=c_ps[:], in1=pb[:], op=ALU.mult)
+        inv_b = sb.tile([P, G], F32, name="inv_b")
+        nc.vector.reciprocal(out=inv_b[:], in_=sum_b[:])
+        dr = sb.tile([P, G], F32, name="dr")
+        nc.vector.tensor_reduce(out=dr[:], in_=pages(drr[:]), axis=AX.X, op=ALU.add)
+        e_over_b = sb.tile([P, G], F32, name="e_over_b")
+        nc.vector.tensor_tensor(out=e_over_b[:], in0=sums[:, :G], in1=inv_b[:], op=ALU.mult)
+        share = sb.tile([P, G], F32, name="share")
+        mu = sb.tile([P, 1], F32, name="mu")
+        nc.vector.scalar_tensor_tensor(
+            out=share[:], in0=dr[:], scalar=r[:], in1=e_over_b[:], op0=ALU.mult, op1=ALU.mult, accum_out=mu[:]
+        )
+        m = sb.tile([P, G], F32, name="m")
+        nc.vector.tensor_tensor(out=m[:], in0=dr[:], in1=inv_b[:], op=ALU.mult)
+
+        ut = sb.tile([P, G], F32, name="ut")
+        beta = sb.tile([P, 1], F32, name="beta")
+        uut = sb.tile([P, G], F32, name="uut")
+        w2 = sb.tile([P, 1], F32, name="w2")
+        beta_sq = sb.tile([P, 1], F32, name="beta_sq")
+        v = sb.tile([P, I], F32, name="v")
+        sq = sb.tile([P, I], F32, name="sq")
+        y = sb.tile([P, I], F32, name="y")
+        res = sb.tile([P, I], F32, name="res")
+        halves = (slice(0, I // 2), slice(I // 2, I))
+
+        def centred_times_e(cols):
+            own = slice(cols.start // PAGE, cols.stop // PAGE)
+            nc.vector.scalar_tensor_tensor(
+                out=pages(v[:, cols]), in0=spread(m[:, own]), scalar=mu[:], in1=pages(e_scaled[:, cols]),
+                op0=ALU.subtract, op1=ALU.mult,
+            )
+            nc.scalar.activation(out=sq[:, cols], in_=v[:, cols], func=ACT.Square, scale=0.5, bias=beta[:])
+
+        nc.vector.scalar_tensor_tensor(
+            out=ut[:], in0=m[:], scalar=mu[:], in1=t_scaled[:], op0=ALU.subtract, op1=ALU.mult, accum_out=beta[:]
+        )
+        nc.scalar.activation(out=beta_sq[:], in_=beta[:], func=ACT.Square)
+        centred_times_e(halves[0])
+        nc.vector.scalar_tensor_tensor(
+            out=uut[:], in0=m[:], scalar=mu[:], in1=ut[:], op0=ALU.subtract, op1=ALU.mult, accum_out=w2[:]
+        )
+        centred_times_e(halves[1])
+        for cols in halves:
+            nc.vector.scalar_tensor_tensor(
+                out=y[:, cols], in0=e_scaled[:, cols], scalar=w2[:], in1=base_sb[:, cols], op0=ALU.mult, op1=ALU.add
+            )
+        for cols in halves:
+            nc.vector.scalar_tensor_tensor(
+                out=res[:, cols], in0=sq[:, cols], scalar=beta_sq[:], in1=y[:, cols], op0=ALU.subtract, op1=ALU.add
+            )
+            nc.sync.dma_start(out=out[:, cols], in_=res[:, cols])

@@ -34,7 +34,7 @@ def tile_attend_gppagethensecond_kernel(
 
         offsets = sb.tile([P, I // 16], U16, name="offsets")
         key_bytes = sb.tile([P, T], U8, name="key_bytes")
-        val_bytes = sb.tile([P, T], U8, name="val_bytes")
+        val_bytes = sb.tile([P, T], U8, name="val_bytes", tag="val_bytes")
         key_words = sb.tile([P, T], I32, name="key_words")
         val_words = sb.tile([P, T], I32, name="val_words", tag="val_words")
         q1_raw = sb.tile([P, PACK * Q], F32, name="q1_raw")
@@ -42,27 +42,28 @@ def tile_attend_gppagethensecond_kernel(
         g_raw = sb.tile([P, PACK * Q], F32, name="g_raw")
         base_sb = sb.tile([P, I], F32, name="base_sb")
 
+        nc.gpsimd.memset(key_bytes[:].bitcast(I32), 0)
         nc.vector.memset(val_bytes[:].bitcast(I32), 0)
         ident = sb.tile([P, P], F32, name="ident")
         make_identity(nc, ident[:])
 
         nc.sync.dma_start(offsets[:], offs)
+        nc.sync.dma_start(out=q1_raw[:], in_=query.rearrange("(p j) w -> p (j w)", j=PACK))
         key_rows = keys_scales[0].bitcast(I32)
         for quad in range(4):
             nc.sync.dma_start(
-                out=key_bytes[32 * quad : 32 * quad + 32, :].bitcast(I32),
-                in_=key_rows[4 * quad : 4 * quad + 4, :].unsqueeze(0).to_broadcast([8, 4, T // 4]),
+                out=key_bytes[32 * quad : 32 * quad + 4, :].bitcast(I32),
+                in_=key_rows[4 * quad : 4 * quad + 4, :],
             )
-        nc.sync.dma_start(out=q1_raw[:], in_=query.rearrange("(p j) w -> p (j w)", j=PACK))
         nc.sync.dma_start(out=key_words[:], in_=keys_words[0].rearrange("p n t -> p (n t)").bitcast(I32))
         nc.sync.dma_start(out=q2_raw[:], in_=query2.rearrange("(p j) w -> p (j w)", j=PACK))
-        nc.sync.dma_start(out=g_raw[:], in_=gout.rearrange("(p j) w -> p (j w)", j=PACK))
         val_rows = vals_scales[0].bitcast(I32)
         for quad in range(4):
             nc.sync.dma_start(
                 out=val_bytes[32 * quad : 32 * quad + 4, :].bitcast(I32),
                 in_=val_rows[4 * quad : 4 * quad + 4, :],
             )
+        nc.sync.dma_start(out=g_raw[:], in_=gout.rearrange("(p j) w -> p (j w)", j=PACK))
         nc.sync.dma_start(out=val_words[:], in_=vals_words[0].rearrange("p n t -> p (n t)").bitcast(I32))
         nc.sync.dma_start(out=base_sb[:], in_=base)
 
@@ -103,6 +104,7 @@ def tile_attend_gppagethensecond_kernel(
         a_ps = product("a_ps", q1_mx, kw, kb)
         q2_mx = quantise("q2", q2_bf)
         b_ps = product("b_ps", q2_mx, kw, kb)
+        nc.vector.tensor_copy(vb[:], val_bytes[:].indirect(offsets[:]))
 
         def pages(ap):
             return ap.rearrange("p (g j) -> p g j", j=PAGE)
@@ -110,24 +112,23 @@ def tile_attend_gppagethensecond_kernel(
         def spread(ap):
             return ap.unsqueeze(2).to_broadcast([P, ap.shape[1], PAGE])
 
-        neg_max = sb.tile([P, 1], F32, name="neg_max")
-        nc.vector.tensor_reduce(out=neg_max[:], in_=a_ps[:], axis=AX.X, op=ALU.max, negate=True)
-        page_max = sb.tile([P, G], F32, name="page_max")
-        nc.vector.tensor_reduce(out=page_max[:], in_=pages(b_ps[:]), axis=AX.X, op=ALU.max)
+        maxima = sb.tile([P, G + 1], F32, name="maxima", tag="val_bytes")
+        page_max, neg_max = maxima[:, :G], maxima[:, G:]
+        nc.vector.tensor_reduce(out=neg_max, in_=a_ps[:], axis=AX.X, op=ALU.max, negate=True)
+        nc.vector.tensor_reduce(out=page_max, in_=pages(b_ps[:]), axis=AX.X, op=ALU.max)
         b_rel = sb.tile([P, I], F32, name="b_rel")
-        nc.vector.tensor_tensor(out=pages(b_rel[:]), in0=pages(b_ps[:]), in1=spread(page_max[:]), op=ALU.subtract)
+        nc.vector.tensor_tensor(out=pages(b_rel[:]), in0=pages(b_ps[:]), in1=spread(page_max), op=ALU.subtract)
 
         ee = sb.tile([P, PAGE, 2 * G], F32, name="ee")
         z = sb.tile([P, 1], F32, name="z")
         nc.scalar.activation(
             out=ee[:, :, :G], in_=a_ps[:].rearrange("p (g j) -> p j g", j=PAGE), func=ACT.Exp,
-            bias=neg_max[:], accum_out=z[:],
+            bias=neg_max, accum_out=z[:],
         )
         nc.scalar.activation(out=ee[:, :, G:], in_=ee[:, :, :G], func=ACT.Square)
         pb = sb.tile([P, I], F32, name="pb")
         nc.scalar.activation(out=pb[:], in_=b_rel[:], func=ACT.Exp)
 
-        nc.vector.tensor_copy(vb[:], val_bytes[:].indirect(offsets[:]))
         g_mx = quantise("g", g_bf)
         nc.vector.tensor_copy(vw[:], val_words[:].bitcast(U32).indirect(offsets[:]))
         c_ps = product("c_ps", g_mx, vw, vb)

import math
from contextlib import ExitStack

import concourse.mybir as mybir
from concourse.masks import make_identity

D, E, T, I, Q, G = 512, 512, 2048, 512, 128, 64
PAGE = I // G
FLOPS = 3 * 2 * 512 * Q * I

F32 = mybir.dt.float32
BF16 = mybir.dt.bfloat16
I32 = mybir.dt.int32
U32 = mybir.dt.uint32
U16 = mybir.dt.uint16
U8 = mybir.dt.uint8
FP8X4 = mybir.dt.float8_e4m3fn_x4
ALU = mybir.AluOpType
ACT = mybir.ActivationFunctionType
AX = mybir.AxisListType

P = 128
PACK = 4
ROOT_C = math.sqrt(512.0 * 2.0 * 512.0)


def tile_attend_gppagethensecond_kernel(
    tc, query, query2, keys_words, keys_scales, gout, vals_words, vals_scales, base, offs, out
):
    nc = tc.nc
    with ExitStack() as ctx:
        sb = ctx.enter_context(tc.tile_pool(name="sb", bufs=1))
        ps = ctx.enter_context(tc.psum_pool(name="ps", bufs=1))

        offsets = sb.tile([P, I // 16], U16, name="offsets")
        key_bytes = sb.tile([P, T], U8, name="key_bytes")
        val_bytes = sb.tile([P, T], U8, name="val_bytes", tag="val_bytes")
        key_words = sb.tile([P, T], I32, name="key_words")
        val_words = sb.tile([P, T], I32, name="val_words", tag="val_words")
        q1_raw = sb.tile([P, PACK * Q], F32, name="q1_raw")
        q2_raw = sb.tile([P, PACK * Q], F32, name="q2_raw")
        g_raw = sb.tile([P, PACK * Q], F32, name="g_raw")
        base_sb = sb.tile([P, I], F32, name="base_sb")

        nc.gpsimd.memset(key_bytes[:].bitcast(I32), 0)
        nc.vector.memset(val_bytes[:].bitcast(I32), 0)
        ident = sb.tile([P, P], F32, name="ident")
        make_identity(nc, ident[:])

        nc.sync.dma_start(offsets[:], offs)
        nc.sync.dma_start(out=q1_raw[:], in_=query.rearrange("(p j) w -> p (j w)", j=PACK))
        key_rows = keys_scales[0].bitcast(I32)
        for quad in range(4):
            nc.sync.dma_start(
                out=key_bytes[32 * quad : 32 * quad + 4, :].bitcast(I32),
                in_=key_rows[4 * quad : 4 * quad + 4, :],
            )
        nc.sync.dma_start(out=key_words[:], in_=keys_words[0].rearrange("p n t -> p (n t)").bitcast(I32))
        nc.sync.dma_start(out=q2_raw[:], in_=query2.rearrange("(p j) w -> p (j w)", j=PACK))
        val_rows = vals_scales[0].bitcast(I32)
        for quad in range(4):
            nc.sync.dma_start(
                out=val_bytes[32 * quad : 32 * quad + 4, :].bitcast(I32),
                in_=val_rows[4 * quad : 4 * quad + 4, :],
            )
        nc.sync.dma_start(out=g_raw[:], in_=gout.rearrange("(p j) w -> p (j w)", j=PACK))
        nc.sync.dma_start(out=val_words[:], in_=vals_words[0].rearrange("p n t -> p (n t)").bitcast(I32))
        nc.sync.dma_start(out=base_sb[:], in_=base)

        def interleave(name, raw):
            grouped = sb.tile([P, Q * PACK], BF16, name=name + "_bf", align_bytes=64)
            nc.scalar.copy(
                out=grouped[:].rearrange("p (w j) -> p w j", j=PACK),
                in_=raw[:].rearrange("p (j w) -> p w j", j=PACK),
            )
            return grouped

        def quantise(name, grouped):
            codes = sb.tile([P, Q], U32, name=name + "_codes", align_bytes=64)
            scales = sb.tile([P, Q], U8, name=name + "_scales", align_bytes=64)
            nc.vector.quantize_mx(out=codes[:].bitcast(FP8X4), scales=scales[:], in_=grouped[:])
            return codes, scales

        def product(name, rows, words, scale_bytes):
            acc = ps.tile([P, I], F32, name=name)
            nc.tensor.matmul_mx(
                out=acc[:], lhsT=rows[0][:].bitcast(FP8X4), lhsT_scale=rows[1][:],
                rhs=words[:].bitcast(FP8X4), rhs_scale=scale_bytes[:], start=True, stop=True,
            )
            return acc

        q1_bf = interleave("q1", q1_raw)
        q2_bf = interleave("q2", q2_raw)
        g_bf = interleave("g", g_raw)

        kb = sb.tile([P, I], U8, name="kb", align_bytes=64)
        kw = sb.tile([P, I], U32, name="kw", align_bytes=64)
        vb = sb.tile([P, I], U8, name="vb", align_bytes=64)
        vw = sb.tile([P, I], U32, name="vw", align_bytes=64)

        nc.vector.tensor_copy(kb[:], key_bytes[:].indirect(offsets[:]))
        q1_mx = quantise("q1", q1_bf)
        nc.vector.tensor_copy(kw[:], key_words[:].bitcast(U32).indirect(offsets[:]))
        a_ps = product("a_ps", q1_mx, kw, kb)
        q2_mx = quantise("q2", q2_bf)
        b_ps = product("b_ps", q2_mx, kw, kb)
        nc.vector.tensor_copy(vb[:], val_bytes[:].indirect(offsets[:]))

        def pages(ap):
            return ap.rearrange("p (g j) -> p g j", j=PAGE)

        def spread(ap):
            return ap.unsqueeze(2).to_broadcast([P, ap.shape[1], PAGE])

        maxima = sb.tile([P, G + 1], F32, name="maxima", tag="val_bytes")
        page_max, neg_max = maxima[:, :G], maxima[:, G:]
        nc.vector.tensor_reduce(out=neg_max, in_=a_ps[:], axis=AX.X, op=ALU.max, negate=True)
        nc.vector.tensor_reduce(out=page_max, in_=pages(b_ps[:]), axis=AX.X, op=ALU.max)
        b_rel = sb.tile([P, I], F32, name="b_rel")
        nc.vector.tensor_tensor(out=pages(b_rel[:]), in0=pages(b_ps[:]), in1=spread(page_max), op=ALU.subtract)

        ee = sb.tile([P, PAGE, 2 * G], F32, name="ee")
        z = sb.tile([P, 1], F32, name="z")
        nc.scalar.activation(
            out=ee[:, :, :G], in_=a_ps[:].rearrange("p (g j) -> p j g", j=PAGE), func=ACT.Exp,
            bias=neg_max, accum_out=z[:],
        )
        nc.scalar.activation(out=ee[:, :, G:], in_=ee[:, :, :G], func=ACT.Square)
        pb = sb.tile([P, I], F32, name="pb")
        nc.scalar.activation(out=pb[:], in_=b_rel[:], func=ACT.Exp)

        g_mx = quantise("g", g_bf)
        nc.vector.tensor_copy(vw[:], val_words[:].bitcast(U32).indirect(offsets[:]))
        c_ps = product("c_ps", g_mx, vw, vb)

        r = sb.tile([P, 1], F32, name="r")
        nc.vector.reciprocal(out=r[:], in_=z[:])
        e_factor = sb.tile([P, 1], F32, name="e_factor")
        t_factor = sb.tile([P, 1], F32, name="t_factor")
        nc.gpsimd.tensor_scalar(out=e_factor[:], in0=r[:], scalar1=-2.0 * ROOT_C, scalar2=1.0, op0=ALU.mult, op1=ALU.mult)
        nc.gpsimd.tensor_scalar(out=t_factor[:], in0=r[:], scalar1=r[:], scalar2=0.5 * ROOT_C, op0=ALU.mult, op1=ALU.mult)
        e_scaled = sb.tile([P, I], F32, name="e_scaled")
        nc.scalar.activation(
            out=pages(e_scaled[:]), in_=ee[:, :, :G].rearrange("p j g -> p g j"), func=ACT.Identity, scale=e_factor[:]
        )

        turned_ps = ps.tile([P, P], F32, name="turned_ps")
        for j in range(PAGE):
            nc.tensor.matmul(
                turned_ps[:], lhsT=ee[:, j, :], rhs=ident[:], is_transpose=True, start=(j == 0), stop=(j == PAGE - 1)
            )
        turned = sb.tile([P, P], F32, name="turned")
        nc.scalar.copy(out=turned[:], in_=turned_ps[:])
        sums = ps.tile([P, 2 * G], F32, name="sums")
        nc.tensor.transpose(sums[:], turned[:], ident[:])
        t_scaled = sb.tile([P, G], F32, name="t_scaled")
        nc.scalar.activation(out=t_scaled[:], in_=sums[:, G:], func=ACT.Identity, scale=t_factor[:])

        sum_b = sb.tile([P, G], F32, name="sum_b", tag="val_words")
        nc.vector.tensor_reduce(out=sum_b[:], in_=pages(pb[:]), axis=AX.X, op=ALU.add)
        drr = sb.tile([P, I], F32, name="drr")
        nc.vector.tensor_tensor(out=drr[:], in0=c_ps[:], in1=pb[:], op=ALU.mult)
        inv_b = sb.tile([P, G], F32, name="inv_b")
        nc.vector.reciprocal(out=inv_b[:], in_=sum_b[:])
        dr = sb.tile([P, G], F32, name="dr")
        nc.vector.tensor_reduce(out=dr[:], in_=pages(drr[:]), axis=AX.X, op=ALU.add)
        e_over_b = sb.tile([P, G], F32, name="e_over_b")
        nc.vector.tensor_tensor(out=e_over_b[:], in0=sums[:, :G], in1=inv_b[:], op=ALU.mult)
        share = sb.tile([P, G], F32, name="share")
        mu = sb.tile([P, 1], F32, name="mu")
        nc.vector.scalar_tensor_tensor(
            out=share[:], in0=dr[:], scalar=r[:], in1=e_over_b[:], op0=ALU.mult, op1=ALU.mult, accum_out=mu[:]
        )
        m = sb.tile([P, G], F32, name="m")
        nc.vector.tensor_tensor(out=m[:], in0=dr[:], in1=inv_b[:], op=ALU.mult)

        ut = sb.tile([P, G], F32, name="ut")
        beta = sb.tile([P, 1], F32, name="beta")
        uut = sb.tile([P, G], F32, name="uut")
        w2 = sb.tile([P, 1], F32, name="w2")
        beta_sq = sb.tile([P, 1], F32, name="beta_sq")
        v = sb.tile([P, I], F32, name="v")
        sq = sb.tile([P, I], F32, name="sq")
        y = sb.tile([P, I], F32, name="y")
        res = sb.tile([P, I], F32, name="res")
        halves = (slice(0, I // 2), slice(I // 2, I))

        def centred_times_e(cols):
            own = slice(cols.start // PAGE, cols.stop // PAGE)
            nc.vector.scalar_tensor_tensor(
                out=pages(v[:, cols]), in0=spread(m[:, own]), scalar=mu[:], in1=pages(e_scaled[:, cols]),
                op0=ALU.subtract, op1=ALU.mult,
            )
            nc.scalar.activation(out=sq[:, cols], in_=v[:, cols], func=ACT.Square, scale=0.5, bias=beta[:])

        nc.vector.scalar_tensor_tensor(
            out=ut[:], in0=m[:], scalar=mu[:], in1=t_scaled[:], op0=ALU.subtract, op1=ALU.mult, accum_out=beta[:]
        )
        nc.scalar.activation(out=beta_sq[:], in_=beta[:], func=ACT.Square)
        centred_times_e(halves[0])
        nc.vector.scalar_tensor_tensor(
            out=uut[:], in0=m[:], scalar=mu[:], in1=ut[:], op0=ALU.subtract, op1=ALU.mult, accum_out=w2[:]
        )
        centred_times_e(halves[1])
        for cols in halves:
            nc.vector.scalar_tensor_tensor(
                out=y[:, cols], in0=e_scaled[:, cols], scalar=w2[:], in1=base_sb[:, cols], op0=ALU.mult, op1=ALU.add
            )
        for cols in halves:
            nc.vector.scalar_tensor_tensor(
                out=res[:, cols], in0=sq[:, cols], scalar=beta_sq[:], in1=y[:, cols], op0=ALU.subtract, op1=ALU.add
            )
            nc.sync.dma_start(out=out[:, cols], in_=res[:, cols])
